import numpy as np
import ml_dtypes


def mxq(x, axis, fmt="e4m3"):
    dtype, down = {"e4m3": (ml_dtypes.float8_e4m3fn, 7), "e5m2": (ml_dtypes.float8_e5m2, 14)}[fmt]
    v = np.moveaxis(np.asarray(x, np.float32).astype(ml_dtypes.bfloat16).astype(np.float64), axis, -1)
    blocks = v.reshape(v.shape[:-1] + (-1, 32))
    amax = np.abs(blocks).max(-1, keepdims=True)
    byte = np.maximum(np.where(amax > 0, np.frexp(amax)[1] - 1 + 127, 0) - down, 1)
    scale = np.exp2(byte - 127.0)
    codes = (blocks / scale).astype(np.float32).astype(dtype).astype(np.float64)
    return np.moveaxis((codes * scale).reshape(v.shape), -1, axis)


WIDE = False


def mx_kscale(k):
    if not WIDE:
        return np.ones(k)
    levels = np.array([10, -10, 5, -5, 0])
    if k % 512:
        return np.exp2(np.random.permutation(np.resize(levels, k // 32))).repeat(32)
    a = np.empty((k // 512, 16))
    for p in range(k // 512):
        a[p, :8] = np.random.permutation(np.resize(levels, 8))
        for g in range(8):
            far = levels[np.abs(levels - a[p, g]) >= 10]
            a[p, g + 8] = far[np.random.randint(len(far))]
    return np.exp2(a.ravel()).repeat(32)


def f64(x):
    return np.asarray(x).astype(np.float64)


def striped(idx):
    return np.tile(idx.reshape(-1, 16).T, (8, 1)).astype(np.uint16)


def unstriped(offs):
    return offs[:16].T.reshape(-1).astype(np.int64)


E2M1 = np.array([0.0, 0.5, 1.0, 1.5, 2.0, 3.0, 4.0, 6.0, -0.0, -0.5, -1.0, -1.5, -2.0, -3.0, -4.0, -6.0])


def pack_weight(w, fmt):
    k, n = w.shape
    w = f64(np.asarray(w, np.float32).astype(ml_dtypes.bfloat16)).reshape(k // 32, 32, n)
    amax = np.abs(w).max(1)
    if fmt == "e4m3":
        byte = np.frexp(amax)[1] - 1 + 127 - 7
    else:
        mant, ex = np.frexp(amax / 6.0)
        byte = np.where(mant > 0.5, ex, ex - 1) + 127
    byte = np.clip(np.where(amax > 0, byte, 1), 1, 254)
    scaled = (w * np.exp2(127.0 - byte)[:, None, :]).reshape(k, n).astype(np.float32)
    by_word = np.ascontiguousarray(scaled.reshape(k // 512, 128, 4, n).transpose(0, 1, 3, 2))
    if fmt == "e4m3":
        words = by_word.astype(ml_dtypes.float8_e4m3fn).view(np.uint8)
    else:
        c = by_word.astype(ml_dtypes.float4_e2m1fn).view(np.uint8) & 0xF
        words = (c[..., 0::2] | (c[..., 1::2] << 4)).reshape(k // 512, 128, 2 * n)
    return np.ascontiguousarray(words), np.ascontiguousarray(byte.astype(np.uint8).reshape(k // 512, 16, n))


def unpack_weight(words, scales, fmt):
    g, _, n = scales.shape
    words = np.ascontiguousarray(words).reshape(g, 128, n, -1)
    if fmt == "e4m3":
        vals = words.view(ml_dtypes.float8_e4m3fn).astype(np.float64)
    else:
        nib = np.empty((g, 128, n, 4), np.uint8)
        nib[..., 0::2] = words & 0xF
        nib[..., 1::2] = words >> 4
        vals = E2M1[nib]
    vals = vals * np.repeat(np.exp2(scales.astype(np.float64) - 127.0), 8, axis=1)[..., None]
    return vals.transpose(0, 1, 3, 2).reshape(g * 512, n)


def gelu(v):
    return 0.5 * v * (1.0 + np.tanh(np.sqrt(2.0 / np.pi) * (v + 0.044715 * v**3)))


K, T, S, S2 = 1024, 2048, 1024, 512

def setup_inputs():
    n = np.random.standard_normal
    s = mx_kscale(K)[:, None]
    leaves = np.random.permutation(T)
    d = {}
    d["tab_words"], d["tab_scales"] = pack_weight(n((K, T)) * s, "e4m3")
    d["offs"] = striped(leaves[:S])
    d["offs2"] = striped(leaves[S:S + S2])
    d["w1"] = (0.53 * n((K, K)) / K ** 0.5 / s).astype(np.float32)
    d["w4_words"], d["w4_scales"] = pack_weight(n((K, K)) / K ** 0.5 / s * s.T, "e2m1")
    d["gain"] = (2.2 * np.exp(0.3 * n(K)) / K ** 0.5 / s[:, 0]).astype(np.float32)
    d["neg"] = (-1.9 * np.exp(0.3 * n(K)) * s[:, 0]).astype(np.float32)
    d["base"] = (0.8 * n((S2, S))).astype(np.float32)
    d["wt"] = (0.4 * np.exp(0.3 * n(S2))).astype(np.float32)
    return d

def reference(tab_words, tab_scales, offs, offs2, w1, w4_words, w4_scales, gain, neg, base, wt):
    TW = unpack_weight(tab_words, tab_scales, "e4m3")
    v = TW[:, unstriped(offs)]
    v2 = TW[:, unstriped(offs2)]
    w1q = mxq(f64(w1), 0, "e4m3")
    w4 = unpack_weight(w4_words, w4_scales, "e2m1")
    h = np.sin(w1q.T @ v) * f64(gain)[:, None]
    low = np.minimum((w1q.T @ v2) * f64(neg)[:, None], w4.T @ v2)
    hq = mxq(h, 0, "e4m3")
    lowq = mxq(low, 0, "e4m3")
    e = v2.T @ hq + lowq.T @ hq
    y = e + f64(base)
    return np.square(y) * f64(wt)[:, None]

@@ -1,0 +1,263 @@
+from contextlib import ExitStack
+
+import concourse.mybir as mybir
+
+K, T, S, S2 = 1024, 2048, 1024, 512
+FLOPS = 2 * K * K * S + 2 * 2 * K * K * S2 + 2 * 2 * K * S2 * S
+
+F32 = mybir.dt.float32
+BF16 = mybir.dt.bfloat16
+I32 = mybir.dt.int32
+U32 = mybir.dt.uint32
+U16 = mybir.dt.uint16
+U8 = mybir.dt.uint8
+FP8X4 = mybir.dt.float8_e4m3fn_x4
+FP4X4 = mybir.dt.float4_e2m1fn_x4
+ALU = mybir.AluOpType
+ACT = mybir.ActivationFunctionType
+
+P = 128
+PACK = 4
+PASS = P * PACK
+NP = K // PASS
+BANK = 512
+HALF = 256
+
+
+def tile_list_watermark_twin_mismatch_kernel(
+    tc, tab_words, tab_scales, offs, offs2, w1, w4_words, w4_scales, gain, neg, base, wt, out
+):
+    nc = tc.nc
+    with ExitStack() as ctx:
+        keep = ctx.enter_context(tc.tile_pool(name="keep", bufs=1))
+        ring = ctx.enter_context(tc.tile_pool(name="ring", bufs=3))
+        psum = ctx.enter_context(tc.psum_pool(name="psum", bufs=4))
+
+        def held(shape, dtype, name):
+            return keep.tile(shape, dtype, name=name, align_bytes=64)
+
+        loose = keep.tile([P, S // 16], U16, name="loose")
+        bound = keep.tile([P, S2 // 16], U16, name="bound")
+        tab_w = [held([P, T], U32, "tab_w%d" % a) for a in range(NP)]
+        tab_s = held([P, T], U8, "tab_s")
+        w4_w = held([P, NP, 2 * K], U8, "w4_w")
+        w4_s = held([P, NP, K], U8, "w4_s")
+        v2_s1 = held([P, S2], U8, "v2_s1")
+        w1_raw = [[held([P, PACK, PASS], F32, "w1_raw%d%d" % (a, b)) for b in range(NP)] for a in range(NP)]
+        gain_t = held([P, NP, PACK], F32, "gain_t")
+        neg_t = held([P, NP, PACK], F32, "neg_t")
+        wt_t = held([P, S2 // P], F32, "wt_t")
+        base_t = [held([P, S], F32, "base%d" % mt) for mt in range(S2 // P)]
+        warm = held([P, 1], F32, "warm")
+        warm_out = held([P, 1], F32, "warm_out")
+
+        nc.vector.memset(tab_s[:].bitcast(I32), 0)
+        nc.vector.memset(warm[:], 0.0)
+        nc.scalar.activation(warm_out[:], warm[:], ACT.Sin)
+        nc.gpsimd.memset(w4_s[:].rearrange("p a n -> p (a n)").bitcast(I32), 0)
+        nc.gpsimd.memset(v2_s1[:].bitcast(I32), 0)
+
+        def load_w1(a, b):
+            rows = w1[a * PASS : (a + 1) * PASS, b * PASS : (b + 1) * PASS]
+            nc.sync.dma_start(w1_raw[a][b][:], rows.rearrange("(p j) c -> p j c", j=PACK))
+
+        def load_tab(a):
+            nc.sync.dma_start(tab_w[a][:].bitcast(I32), tab_words[a].rearrange("p t i -> p (t i)").bitcast(I32))
+
+        nc.sync.dma_start(bound[:], offs2)
+        nc.sync.dma_start(loose[:], offs)
+        load_tab(0)
+        for q in range(4):
+            nc.sync.dma_start(
+                tab_s[32 * q : 32 * q + 4 * NP, :].bitcast(I32), tab_scales[:, 4 * q : 4 * q + 4, :].bitcast(I32)
+            )
+        load_tab(1)
+        nc.sync.dma_start(w4_w[:].bitcast(I32), w4_words.rearrange("a p n -> p a n").bitcast(I32))
+        for q in range(4):
+            nc.sync.dma_start(
+                w4_s[32 * q : 32 * q + 4, :, :].bitcast(I32),
+                w4_scales[:, 4 * q : 4 * q + 4, :].rearrange("a r n -> r a n").bitcast(I32),
+            )
+        load_w1(0, 0)
+        nc.sync.dma_start(gain_t[:], gain.rearrange("(b p t) -> p b t", b=NP, t=PACK))
+        nc.sync.dma_start(neg_t[:], neg.rearrange("(b p t) -> p b t", b=NP, t=PACK))
+        load_w1(1, 0)
+        load_w1(0, 1)
+        load_w1(1, 1)
+        for mt in range(S2 // P):
+            nc.sync.dma_start(base_t[mt][:], base[mt * P : (mt + 1) * P, :])
+        with nc.allow_non_contiguous_dma(reason="one weight a partition"):
+            nc.sync.dma_start(wt_t[:], wt.rearrange("(mt p) -> p mt", p=P))
+
+        v2_w = [held([P, S2], U32, "v2_w%d" % a) for a in range(NP)]
+        v2_s = held([P, S2], U8, "v2_s")
+        v_w = [[held([P, BANK], U32, "v_w%d0" % a)] for a in range(NP)]
+        v_s = [held([P, BANK], U8, "v_s0")]
+
+        def part(jc):
+            return loose[:, jc * 32 : (jc + 1) * 32]
+
+        nc.vector.tensor_copy(v2_s[:], tab_s[:].indirect(bound[:]))
+        for q in range(4):
+            nc.gpsimd.dma_start(
+                v2_s1[32 * q : 32 * q + 4, :].bitcast(I32), v2_s[32 * q + 4 : 32 * q + 8, :].bitcast(I32)
+            )
+        nc.vector.tensor_copy(v_s[0][:], tab_s[:].indirect(part(0)))
+        for a in range(NP):
+            nc.vector.tensor_copy(v_w[a][0][:], tab_w[a][:].indirect(part(0)))
+            nc.vector.tensor_copy(v2_w[a][:], tab_w[a][:].indirect(bound[:]))
+        v2_planes = [v2_s[:], v2_s1[:]]
+
+        w4_wd = held([P, NP, PACK, 2 * (K // PACK)], U8, "w4_wd")
+        w4_sd = held([P, NP, PACK, K // PACK], U8, "w4_sd")
+        nc.vector.tensor_copy(
+            w4_wd[:].bitcast(U16), w4_w[:].bitcast(U16).rearrange("p a (c t) -> p a t c", t=PACK)
+        )
+        nc.vector.tensor_copy(w4_sd[:], w4_s[:].rearrange("p a (c t) -> p a t c", t=PACK))
+
+        w1_q = [[held([P, PASS], U32, "w1_q%d%d" % (a, b)) for b in range(NP)] for a in range(NP)]
+        w1_s = [[held([P, PASS], U8, "w1_s%d%d" % (a, b)) for b in range(NP)] for a in range(NP)]
+
+        def quant_w1(a, b):
+            for u in range(2):
+                g = keep.tile([P, 2, P, PACK], BF16, name="w1_g", tag="g%d%d%d" % (a, b, u), align_bytes=64)
+                nc.scalar.copy(
+                    g[:].rearrange("p t m j -> p m j t"),
+                    w1_raw[a][b][:].rearrange("p j (m t) -> p m j t", t=PACK)[:, :, :, 2 * u : 2 * u + 2],
+                )
+                cols = slice(u * HALF, (u + 1) * HALF)
+                nc.vector.quantize_mx(
+                    out=w1_q[a][b][:, cols].bitcast(FP8X4),
+                    scales=w1_s[a][b][:, cols],
+                    in_=g[:].rearrange("p t m j -> p (t m j)"),
+                )
+
+        h_q = [[held([P, BANK], U32, "h_q%d%d" % (b, jc)) for jc in range(2)] for b in range(NP)]
+        h_s = [[held([P, BANK], U8, "h_s%d%d" % (b, jc)) for jc in range(2)] for b in range(NP)]
+        low_q = [held([P, S2], U32, "low_q%d" % b) for b in range(NP)]
+        low_s = [held([P, S2], U8, "low_s%d" % b) for b in range(NP)]
+
+        def h_unit(b, jc, half):
+            cols = slice(half * HALF, (half + 1) * HALF)
+            sines = ring.tile([P, PACK, HALF], F32, name="sines")
+            for pair in range(2):
+                acc = psum.tile([P, 2, HALF], F32, name="sc")
+                for tt in range(2):
+                    t = 2 * pair + tt
+                    for a in range(NP):
+                        nc.tensor.matmul_mx(
+                            out=acc[:, tt, :],
+                            lhsT=w1_q[a][b][:, t * P : (t + 1) * P].bitcast(FP8X4),
+                            lhsT_scale=w1_s[a][b][:, t * P : (t + 1) * P],
+                            rhs=v_w[a][jc][:, cols].bitcast(FP8X4),
+                            rhs_scale=v_s[jc][4 * a : P, cols],
+                            start=(a == 0),
+                            stop=(a == NP - 1),
+                        )
+                nc.scalar.activation(sines[:, 2 * pair : 2 * pair + 2, :], acc[:], ACT.Sin)
+            g = ring.tile([P, HALF, PACK], BF16, name="h_g", align_bytes=64)
+            nc.vector.tensor_tensor(
+                g[:].rearrange("p (c i) t -> p c t i", i=4),
+                sines[:].rearrange("p t (c i) -> p c t i", i=4),
+                gain_t[:, b, :].unsqueeze(1).unsqueeze(3).to_broadcast([P, HALF // 4, PACK, 4]),
+                ALU.mult,
+            )
+            nc.vector.quantize_mx(
+                out=h_q[b][jc][:, cols].bitcast(FP8X4),
+                scales=h_s[b][jc][:, cols],
+                in_=g[:].rearrange("p n t -> p (n t)"),
+            )
+
+        def low_unit(b):
+            second = []
+            for mt in range(S2 // P):
+                acc = psum.tile([P, PACK, P], F32, name="vb")
+                cols = slice(mt * P, (mt + 1) * P)
+                for t in range(PACK):
+                    for a in range(NP):
+                        nc.tensor.matmul_mx(
+                            out=acc[:, t, :],
+                            lhsT=w4_wd[:, a, t, 2 * b * P : 2 * (b + 1) * P].bitcast(FP4X4),
+                            lhsT_scale=w4_sd[:, a, t, b * P : (b + 1) * P],
+                            rhs=v2_w[a][:, cols].bitcast(FP8X4),
+                            rhs_scale=v2_planes[a][:, cols],
+                            start=(a == 0),
+                            stop=(a == NP - 1),
+                        )
+                second.append(acc)
+            first = ring.tile([P, PACK, S2], F32, name="first", bufs=2)
+            for t in range(PACK):
+                acc = psum.tile([P, S2], F32, name="sc")
+                for a in range(NP):
+                    nc.tensor.matmul_mx(
+                        out=acc[:],
+                        lhsT=w1_q[a][b][:, t * P : (t + 1) * P].bitcast(FP8X4),
+                        lhsT_scale=w1_s[a][b][:, t * P : (t + 1) * P],
+                        rhs=v2_w[a][:].bitcast(FP8X4),
+                        rhs_scale=v2_planes[a],
+                        start=(a == 0),
+                        stop=(a == NP - 1),
+                    )
+                nc.scalar.activation(first[:, t, :], acc[:], ACT.Copy, scale=neg_t[:, b, t : t + 1])
+            g = ring.tile([P, S2, PACK], BF16, name="low_g", align_bytes=64, bufs=2)
+            for mt in range(S2 // P):
+                cols = slice(mt * P, (mt + 1) * P)
+                nc.vector.tensor_tensor(
+                    g[:, cols, :].rearrange("p (c i) t -> p c t i", i=4),
+                    second[mt][:].rearrange("p t (c i) -> p c t i", i=4),
+                    first[:, :, cols].rearrange("p t (c i) -> p c t i", i=4),
+                    ALU.min,
+                )
+            for half in range(2):
+                cols = slice(half * HALF, (half + 1) * HALF)
+                nc.vector.quantize_mx(
+                    out=low_q[b][:, cols].bitcast(FP8X4),
+                    scales=low_s[b][:, cols],
+                    in_=g[:, cols, :].rearrange("p n t -> p (n t)"),
+                )
+
+        def final(mt, jc):
+            cols = slice(mt * P, (mt + 1) * P)
+            acc = psum.tile([P, BANK], F32, name="vb")
+            for b in range(NP):
+                for which in range(2):
+                    codes, plane = (v2_w[b], v2_planes[b]) if which == 0 else (low_q[b], low_s[b][:])
+                    nc.tensor.matmul_mx(
+                        out=acc[:],
+                        lhsT=codes[:, cols].bitcast(FP8X4),
+                        lhsT_scale=plane[:, cols],
+                        rhs=h_q[b][jc][:].bitcast(FP8X4),
+                        rhs_scale=h_s[b][jc][:],
+                        start=(b == 0 and which == 0),
+                        stop=(b == NP - 1 and which == 1),
+                    )
+            y = ring.tile([P, BANK], F32, name="y")
+            nc.vector.tensor_tensor(y[:], acc[:], base_t[mt][:, jc * BANK : (jc + 1) * BANK], ALU.add)
+            sq = ring.tile([P, BANK], F32, name="sq")
+            nc.scalar.activation(sq[:], y[:], ACT.Square)
+            res = ring.tile([P, BANK], F32, name="res", bufs=4)
+            nc.vector.tensor_scalar(res[:], sq[:], wt_t[:, mt : mt + 1], None, ALU.mult)
+            nc.sync.dma_start(out[cols, jc * BANK : (jc + 1) * BANK], res[:])
+
+        quant_w1(0, 0)
+        quant_w1(1, 0)
+        v_s.append(keep.tile([P, BANK], U8, name="v_s1", tag="g001", align_bytes=64))
+        nc.vector.tensor_copy(v_s[1][:], tab_s[:].indirect(part(1)))
+        for a in range(NP):
+            v_w[a].append(keep.tile([P, BANK], U32, name="v_w1", tag="g10%d" % a, align_bytes=64))
+            nc.vector.tensor_copy(v_w[a][1][:], tab_w[a][:].indirect(part(1)))
+        h_unit(0, 0, 0)
+        h_unit(0, 0, 1)
+        quant_w1(0, 1)
+        low_unit(0)
+        quant_w1(1, 1)
+        h_unit(0, 1, 0)
+        h_unit(0, 1, 1)
+        low_unit(1)
+        h_unit(1, 0, 0)
+        h_unit(1, 0, 1)
+        h_unit(1, 1, 0)
+        h_unit(1, 1, 1)
+        for jc in range(2):
+            for mt in range(S2 // P):
+                final(mt, jc)

@@ -19,9 +19,14 @@ ACT = mybir.ActivationFunctionType
 P = 128
 PACK = 4
 PASS = P * PACK
-NP = K // PASS
+PASSES = K // PASS
+QUADS = 4
+ROWS = 4
 BANK = 512
-HALF = 256
+HALF = BANK // 2
+RUN = 4
+M_TILES = S2 // P
+GAIN_ON_SCALAR = (1, 1, 1)
 
 
 def tile_list_watermark_twin_mismatch_kernel(
@@ -30,7 +35,7 @@ def tile_list_watermark_twin_mismatch_kernel(
     nc = tc.nc
     with ExitStack() as ctx:
         keep = ctx.enter_context(tc.tile_pool(name="keep", bufs=1))
-        ring = ctx.enter_context(tc.tile_pool(name="ring", bufs=3))
+        ring = ctx.enter_context(tc.tile_pool(name="ring", bufs=4))
         psum = ctx.enter_context(tc.psum_pool(name="psum", bufs=4))
 
         def held(shape, dtype, name):
@@ -38,226 +43,256 @@ def tile_list_watermark_twin_mismatch_kernel(
 
         loose = keep.tile([P, S // 16], U16, name="loose")
         bound = keep.tile([P, S2 // 16], U16, name="bound")
-        tab_w = [held([P, T], U32, "tab_w%d" % a) for a in range(NP)]
+        tab_w = [held([P, T], U32, "tab_w%d" % a) for a in range(PASSES)]
         tab_s = held([P, T], U8, "tab_s")
-        w4_w = held([P, NP, 2 * K], U8, "w4_w")
-        w4_s = held([P, NP, K], U8, "w4_s")
-        v2_s1 = held([P, S2], U8, "v2_s1")
-        w1_raw = [[held([P, PACK, PASS], F32, "w1_raw%d%d" % (a, b)) for b in range(NP)] for a in range(NP)]
-        gain_t = held([P, NP, PACK], F32, "gain_t")
-        neg_t = held([P, NP, PACK], F32, "neg_t")
-        wt_t = held([P, S2 // P], F32, "wt_t")
-        base_t = [held([P, S], F32, "base%d" % mt) for mt in range(S2 // P)]
-        warm = held([P, 1], F32, "warm")
+        w4_w = held([P, PASSES, 2 * K], U8, "w4_w")
+        w4_s = held([P, PASSES, K], U8, "w4_s")
+        w4_wd = held([P, PASSES, PACK, 2 * (K // PACK)], U8, "w4_wd")
+        w4_sd = held([P, PASSES, PACK, K // PACK], U8, "w4_sd")
+        bound_w = [held([P, S2], U32, "bound_w%d" % a) for a in range(PASSES)]
+        bound_s = [held([P, S2], U8, "bound_s%d" % a) for a in range(PASSES)]
+        loose_w = [[held([P, BANK], U32, "loose_w%d%d" % (a, jc)) for jc in range(2)] for a in range(PASSES)]
+        loose_s = [held([P, BANK], U8, "loose_s%d" % jc) for jc in range(2)]
+        w1_q = [[held([P, PASS], U32, "w1_q%d%d" % (a, b)) for b in range(PASSES)] for a in range(PASSES)]
+        w1_s = [[held([P, PASS], U8, "w1_s%d%d" % (a, b)) for b in range(PASSES)] for a in range(PASSES)]
+        h_q = [[held([P, BANK], U32, "h_q%d%d" % (b, jc)) for jc in range(2)] for b in range(PASSES)]
+        h_s = [[held([P, BANK], U8, "h_s%d%d" % (b, jc)) for jc in range(2)] for b in range(PASSES)]
+        low_q = [held([P, S2], U32, "low_q%d" % b) for b in range(PASSES)]
+        low_s = [held([P, S2], U8, "low_s%d" % b) for b in range(PASSES)]
+        gain_t = held([P, PASSES, PACK], F32, "gain_t")
+        neg_t = held([P, PASSES, PACK], F32, "neg_t")
+        wt_t = held([P, M_TILES], F32, "wt_t")
+        base_t = [held([P, S], F32, "base%d" % mt) for mt in range(M_TILES)]
+        warm_in = held([P, 1], F32, "warm_in")
         warm_out = held([P, 1], F32, "warm_out")
+        w1_raw = {}
+        w1_grouped = [
+            [held([P, PACK, P, PACK], BF16, "w1_grouped%d%d" % (a, b)) for b in range(PASSES)] for a in range(PASSES)
+        ]
 
         nc.vector.memset(tab_s[:].bitcast(I32), 0)
-        nc.vector.memset(warm[:], 0.0)
-        nc.scalar.activation(warm_out[:], warm[:], ACT.Sin)
-        nc.gpsimd.memset(w4_s[:].rearrange("p a n -> p (a n)").bitcast(I32), 0)
-        nc.gpsimd.memset(v2_s1[:].bitcast(I32), 0)
+        nc.vector.memset(warm_in[:], 0.0)
+        nc.scalar.activation(warm_out[:], warm_in[:], ACT.Sin)
+        nc.vector.memset(w4_s[:].rearrange("p a n -> p (a n)").bitcast(I32), 0)
+        nc.vector.memset(bound_s[1][:].bitcast(I32), 0)
 
-        def load_w1(a, b):
-            rows = w1[a * PASS : (a + 1) * PASS, b * PASS : (b + 1) * PASS]
-            nc.sync.dma_start(w1_raw[a][b][:], rows.rearrange("(p j) c -> p j c", j=PACK))
+        def load_planes(tile, scales):
+            for q in range(QUADS):
+                rows = tile[32 * q : 32 * q + ROWS * PASSES, :]
+                nc.sync.dma_start(rows.bitcast(I32), scales[:, ROWS * q : ROWS * (q + 1), :].bitcast(I32))
+
+        def lift_plane(lifted, both):
+            for q in range(QUADS):
+                nc.sync.dma_start(
+                    lifted[32 * q : 32 * q + ROWS].bitcast(I32), both[32 * q + ROWS : 32 * q + 2 * ROWS].bitcast(I32)
+                )
 
         def load_tab(a):
             nc.sync.dma_start(tab_w[a][:].bitcast(I32), tab_words[a].rearrange("p t i -> p (t i)").bitcast(I32))
 
+        def load_w1(a, b, half):
+            raw = held([P, PACK, HALF], F32, "w1_raw%d%d%d" % (a, b, half))
+            first_col = b * PASS + half * HALF
+            block = w1[a * PASS : (a + 1) * PASS, first_col : first_col + HALF]
+            nc.sync.dma_start(raw[:], block.rearrange("(p i) c -> p i c", i=PACK))
+            w1_raw[(a, b, half)] = raw
+
+        def gather(picked, window, offsets):
+            nc.vector.tensor_copy(picked[:], window[:].indirect(offsets))
+
+        def loose_part(jc):
+            return loose[:, jc * (BANK // 16) : (jc + 1) * (BANK // 16)]
+
         nc.sync.dma_start(bound[:], offs2)
+        load_planes(tab_s, tab_scales)
         nc.sync.dma_start(loose[:], offs)
         load_tab(0)
-        for q in range(4):
-            nc.sync.dma_start(
-                tab_s[32 * q : 32 * q + 4 * NP, :].bitcast(I32), tab_scales[:, 4 * q : 4 * q + 4, :].bitcast(I32)
-            )
+        load_w1(0, 0, 0)
+        load_w1(0, 0, 1)
+        for q in range(QUADS):
+            rows = w4_scales[:, ROWS * q : ROWS * (q + 1), :].rearrange("a r n -> r a n")
+            nc.sync.dma_start(w4_s[32 * q : 32 * q + ROWS, :, :].bitcast(I32), rows.bitcast(I32))
+        load_w1(1, 0, 0)
+        load_w1(1, 0, 1)
         load_tab(1)
+        gather(bound_s[0], tab_s, bound[:])
+        lift_plane(bound_s[1], bound_s[0])
+        load_w1(0, 1, 0)
+        nc.vector.tensor_copy(w4_sd[:], w4_s[:].rearrange("p a (c t) -> p a t c", t=PACK))
         nc.sync.dma_start(w4_w[:].bitcast(I32), w4_words.rearrange("a p n -> p a n").bitcast(I32))
-        for q in range(4):
-            nc.sync.dma_start(
-                w4_s[32 * q : 32 * q + 4, :, :].bitcast(I32),
-                w4_scales[:, 4 * q : 4 * q + 4, :].rearrange("a r n -> r a n").bitcast(I32),
-            )
-        load_w1(0, 0)
-        nc.sync.dma_start(gain_t[:], gain.rearrange("(b p t) -> p b t", b=NP, t=PACK))
-        nc.sync.dma_start(neg_t[:], neg.rearrange("(b p t) -> p b t", b=NP, t=PACK))
-        load_w1(1, 0)
-        load_w1(0, 1)
-        load_w1(1, 1)
-        for mt in range(S2 // P):
+        nc.sync.dma_start(gain_t[:], gain.rearrange("(b p t) -> p b t", b=PASSES, t=PACK))
+        nc.sync.dma_start(neg_t[:], neg.rearrange("(b p t) -> p b t", b=PASSES, t=PACK))
+        load_w1(0, 1, 1)
+        load_w1(1, 1, 0)
+        load_w1(1, 1, 1)
+        for mt in range(M_TILES):
             nc.sync.dma_start(base_t[mt][:], base[mt * P : (mt + 1) * P, :])
         with nc.allow_non_contiguous_dma(reason="one weight a partition"):
             nc.sync.dma_start(wt_t[:], wt.rearrange("(mt p) -> p mt", p=P))
 
-        v2_w = [held([P, S2], U32, "v2_w%d" % a) for a in range(NP)]
-        v2_s = held([P, S2], U8, "v2_s")
-        v_w = [[held([P, BANK], U32, "v_w%d0" % a)] for a in range(NP)]
-        v_s = [held([P, BANK], U8, "v_s0")]
-
-        def part(jc):
-            return loose[:, jc * 32 : (jc + 1) * 32]
-
-        nc.vector.tensor_copy(v2_s[:], tab_s[:].indirect(bound[:]))
-        for q in range(4):
-            nc.gpsimd.dma_start(
-                v2_s1[32 * q : 32 * q + 4, :].bitcast(I32), v2_s[32 * q + 4 : 32 * q + 8, :].bitcast(I32)
+        def cast_w1(a, b, half):
+            nc.scalar.copy(
+                w1_grouped[a][b][:].rearrange("p t c i -> p c i t")[:, half * P // 2 : (half + 1) * P // 2, :, :],
+                w1_raw[(a, b, half)][:].rearrange("p i (c t) -> p c i t", t=PACK),
             )
-        nc.vector.tensor_copy(v_s[0][:], tab_s[:].indirect(part(0)))
-        for a in range(NP):
-            nc.vector.tensor_copy(v_w[a][0][:], tab_w[a][:].indirect(part(0)))
-            nc.vector.tensor_copy(v2_w[a][:], tab_w[a][:].indirect(bound[:]))
-        v2_planes = [v2_s[:], v2_s1[:]]
 
-        w4_wd = held([P, NP, PACK, 2 * (K // PACK)], U8, "w4_wd")
-        w4_sd = held([P, NP, PACK, K // PACK], U8, "w4_sd")
-        nc.vector.tensor_copy(
-            w4_wd[:].bitcast(U16), w4_w[:].bitcast(U16).rearrange("p a (c t) -> p a t c", t=PACK)
-        )
-        nc.vector.tensor_copy(w4_sd[:], w4_s[:].rearrange("p a (c t) -> p a t c", t=PACK))
-
-        w1_q = [[held([P, PASS], U32, "w1_q%d%d" % (a, b)) for b in range(NP)] for a in range(NP)]
-        w1_s = [[held([P, PASS], U8, "w1_s%d%d" % (a, b)) for b in range(NP)] for a in range(NP)]
-
-        def quant_w1(a, b):
-            for u in range(2):
-                g = keep.tile([P, 2, P, PACK], BF16, name="w1_g", tag="g%d%d%d" % (a, b, u), align_bytes=64)
-                nc.scalar.copy(
-                    g[:].rearrange("p t m j -> p m j t"),
-                    w1_raw[a][b][:].rearrange("p j (m t) -> p m j t", t=PACK)[:, :, :, 2 * u : 2 * u + 2],
-                )
-                cols = slice(u * HALF, (u + 1) * HALF)
+        def quantise_w1(a, b):
+            grouped = w1_grouped[a][b]
+            for half in range(2):
+                cols = slice(half * HALF, (half + 1) * HALF)
                 nc.vector.quantize_mx(
                     out=w1_q[a][b][:, cols].bitcast(FP8X4),
                     scales=w1_s[a][b][:, cols],
-                    in_=g[:].rearrange("p t m j -> p (t m j)"),
+                    in_=grouped[:, 2 * half : 2 * half + 2, :, :].rearrange("p t c i -> p (t c i)"),
                 )
 
-        h_q = [[held([P, BANK], U32, "h_q%d%d" % (b, jc)) for jc in range(2)] for b in range(NP)]
-        h_s = [[held([P, BANK], U8, "h_s%d%d" % (b, jc)) for jc in range(2)] for b in range(NP)]
-        low_q = [held([P, S2], U32, "low_q%d" % b) for b in range(NP)]
-        low_s = [held([P, S2], U8, "low_s%d" % b) for b in range(NP)]
+        def w1_product(acc, b, t, words, planes):
+            for a in range(PASSES):
+                nc.tensor.matmul_mx(
+                    out=acc,
+                    lhsT=w1_q[a][b][:, t * P : (t + 1) * P].bitcast(FP8X4),
+                    lhsT_scale=w1_s[a][b][:, t * P : (t + 1) * P],
+                    rhs=words[a].bitcast(FP8X4),
+                    rhs_scale=planes[ROWS * a : P],
+                    start=(a == 0),
+                    stop=(a == PASSES - 1),
+                )
 
-        def h_unit(b, jc, half):
+        def woven(tile):
+            return tile.rearrange("p (c i) t -> p c t i", i=RUN)
+
+        def by_slice(tile):
+            return tile.rearrange("p t (c i) -> p c t i", i=RUN)
+
+        def finish_h(sines, b, jc, half):
             cols = slice(half * HALF, (half + 1) * HALF)
-            sines = ring.tile([P, PACK, HALF], F32, name="sines")
-            for pair in range(2):
-                acc = psum.tile([P, 2, HALF], F32, name="sc")
-                for tt in range(2):
-                    t = 2 * pair + tt
-                    for a in range(NP):
-                        nc.tensor.matmul_mx(
-                            out=acc[:, tt, :],
-                            lhsT=w1_q[a][b][:, t * P : (t + 1) * P].bitcast(FP8X4),
-                            lhsT_scale=w1_s[a][b][:, t * P : (t + 1) * P],
-                            rhs=v_w[a][jc][:, cols].bitcast(FP8X4),
-                            rhs_scale=v_s[jc][4 * a : P, cols],
-                            start=(a == 0),
-                            stop=(a == NP - 1),
-                        )
-                nc.scalar.activation(sines[:, 2 * pair : 2 * pair + 2, :], acc[:], ACT.Sin)
-            g = ring.tile([P, HALF, PACK], BF16, name="h_g", align_bytes=64)
-            nc.vector.tensor_tensor(
-                g[:].rearrange("p (c i) t -> p c t i", i=4),
-                sines[:].rearrange("p t (c i) -> p c t i", i=4),
-                gain_t[:, b, :].unsqueeze(1).unsqueeze(3).to_broadcast([P, HALF // 4, PACK, 4]),
-                ALU.mult,
-            )
+            grouped = ring.tile([P, HALF, PACK], BF16, name="h_grouped", align_bytes=64)
+            if (b, jc, half) == GAIN_ON_SCALAR:
+                scaled = held([P, PACK, HALF], BF16, "scaled")
+                for t in range(PACK):
+                    nc.scalar.activation(scaled[:, t, :], sines[:, t, :], ACT.Copy, scale=gain_t[:, b, t : t + 1])
+                nc.scalar.copy(woven(grouped[:]), by_slice(scaled[:]))
+            else:
+                gains = gain_t[:, b, :].unsqueeze(1).unsqueeze(3).to_broadcast([P, HALF // RUN, PACK, RUN])
+                nc.vector.tensor_tensor(woven(grouped[:]), by_slice(sines), gains, ALU.mult)
             nc.vector.quantize_mx(
                 out=h_q[b][jc][:, cols].bitcast(FP8X4),
                 scales=h_s[b][jc][:, cols],
-                in_=g[:].rearrange("p n t -> p (n t)"),
+                in_=grouped[:].rearrange("p n t -> p (n t)"),
             )
 
-        def low_unit(b):
-            second = []
-            for mt in range(S2 // P):
-                acc = psum.tile([P, PACK, P], F32, name="vb")
+        def first_h():
+            sines = held([P, PACK, BANK], F32, "w1_raw010")
+            for t in range(PACK):
+                acc = psum.tile([P, BANK], F32, name="left")
+                w1_product(acc[:], 0, t, [loose_w[a][0][:] for a in range(PASSES)], loose_s[0][:])
+                nc.scalar.activation(sines[:, t, :], acc[:], ACT.Sin)
+            for half in range(2):
+                finish_h(sines[:, :, half * HALF : (half + 1) * HALF], 0, 0, half)
+
+        def later_h(b, jc):
+            for half in range(2):
+                cols = slice(half * HALF, (half + 1) * HALF)
+                sines = ring.tile([P, PACK, HALF], F32, name="sines", bufs=5)
+                for pair in range(2):
+                    acc = psum.tile([P, 2, HALF], F32, name="left")
+                    for t in (2 * pair, 2 * pair + 1):
+                        words = [loose_w[a][jc][:, cols] for a in range(PASSES)]
+                        w1_product(acc[:, t % 2, :], b, t, words, loose_s[jc][:, cols])
+                    nc.scalar.activation(sines[:, 2 * pair : 2 * pair + 2, :], acc[:], ACT.Sin)
+                finish_h(sines[:], b, jc, half)
+
+        def make_low(b, w1_banks):
+            negated = ring.tile([P, PACK, S2], F32, name="negated", bufs=2)
+            for t in range(PACK):
+                acc = psum.tile([P, S2], F32, name=w1_banks)
+                w1_product(acc[:], b, t, [bound_w[a][:] for a in range(PASSES)], bound_s[0][:])
+                nc.scalar.activation(negated[:, t, :], acc[:], ACT.Copy, scale=neg_t[:, b, t : t + 1])
+            w4_sums = []
+            for mt in range(M_TILES):
+                acc = psum.tile([P, PACK, P], F32, name="right")
                 cols = slice(mt * P, (mt + 1) * P)
                 for t in range(PACK):
-                    for a in range(NP):
+                    for a in range(PASSES):
                         nc.tensor.matmul_mx(
                             out=acc[:, t, :],
                             lhsT=w4_wd[:, a, t, 2 * b * P : 2 * (b + 1) * P].bitcast(FP4X4),
                             lhsT_scale=w4_sd[:, a, t, b * P : (b + 1) * P],
-                            rhs=v2_w[a][:, cols].bitcast(FP8X4),
-                            rhs_scale=v2_planes[a][:, cols],
+                            rhs=bound_w[a][:, cols].bitcast(FP8X4),
+                            rhs_scale=bound_s[a][:, cols],
                             start=(a == 0),
-                            stop=(a == NP - 1),
+                            stop=(a == PASSES - 1),
                         )
-                second.append(acc)
-            first = ring.tile([P, PACK, S2], F32, name="first", bufs=2)
-            for t in range(PACK):
-                acc = psum.tile([P, S2], F32, name="sc")
-                for a in range(NP):
-                    nc.tensor.matmul_mx(
-                        out=acc[:],
-                        lhsT=w1_q[a][b][:, t * P : (t + 1) * P].bitcast(FP8X4),
-                        lhsT_scale=w1_s[a][b][:, t * P : (t + 1) * P],
-                        rhs=v2_w[a][:].bitcast(FP8X4),
-                        rhs_scale=v2_planes[a],
-                        start=(a == 0),
-                        stop=(a == NP - 1),
-                    )
-                nc.scalar.activation(first[:, t, :], acc[:], ACT.Copy, scale=neg_t[:, b, t : t + 1])
-            g = ring.tile([P, S2, PACK], BF16, name="low_g", align_bytes=64, bufs=2)
-            for mt in range(S2 // P):
+                w4_sums.append(acc)
+            grouped = ring.tile([P, S2, PACK], BF16, name="low_grouped", bufs=2, align_bytes=64)
+            for mt in range(M_TILES):
                 cols = slice(mt * P, (mt + 1) * P)
                 nc.vector.tensor_tensor(
-                    g[:, cols, :].rearrange("p (c i) t -> p c t i", i=4),
-                    second[mt][:].rearrange("p t (c i) -> p c t i", i=4),
-                    first[:, :, cols].rearrange("p t (c i) -> p c t i", i=4),
-                    ALU.min,
+                    woven(grouped[:, cols, :]), by_slice(w4_sums[mt][:]), by_slice(negated[:, :, cols]), ALU.min
                 )
             for half in range(2):
                 cols = slice(half * HALF, (half + 1) * HALF)
                 nc.vector.quantize_mx(
                     out=low_q[b][:, cols].bitcast(FP8X4),
                     scales=low_s[b][:, cols],
-                    in_=g[:, cols, :].rearrange("p n t -> p (n t)"),
+                    in_=grouped[:, cols, :].rearrange("p n t -> p (n t)"),
                 )
 
-        def final(mt, jc):
-            cols = slice(mt * P, (mt + 1) * P)
-            acc = psum.tile([P, BANK], F32, name="vb")
-            for b in range(NP):
-                for which in range(2):
-                    codes, plane = (v2_w[b], v2_planes[b]) if which == 0 else (low_q[b], low_s[b][:])
-                    nc.tensor.matmul_mx(
-                        out=acc[:],
-                        lhsT=codes[:, cols].bitcast(FP8X4),
-                        lhsT_scale=plane[:, cols],
-                        rhs=h_q[b][jc][:].bitcast(FP8X4),
-                        rhs_scale=h_s[b][jc][:],
-                        start=(b == 0 and which == 0),
-                        stop=(b == NP - 1 and which == 1),
-                    )
-            y = ring.tile([P, BANK], F32, name="y")
-            nc.vector.tensor_tensor(y[:], acc[:], base_t[mt][:, jc * BANK : (jc + 1) * BANK], ALU.add)
-            sq = ring.tile([P, BANK], F32, name="sq")
-            nc.scalar.activation(sq[:], y[:], ACT.Square)
-            res = ring.tile([P, BANK], F32, name="res", bufs=4)
-            nc.vector.tensor_scalar(res[:], sq[:], wt_t[:, mt : mt + 1], None, ALU.mult)
-            nc.sync.dma_start(out[cols, jc * BANK : (jc + 1) * BANK], res[:])
+        def score(first_col, width, banks):
+            jc = first_col // BANK
+            h_cols = slice(first_col % BANK, first_col % BANK + width)
+            out_cols = slice(first_col, first_col + width)
+            for mt in range(M_TILES):
+                rows = slice(mt * P, (mt + 1) * P)
+                acc = psum.tile([P, width], F32, name=banks)
+                for b in range(PASSES):
+                    sides = ((bound_w[b], bound_s[0][ROWS * b : P]), (low_q[b], low_s[b][:]))
+                    for side, (words, plane) in enumerate(sides):
+                        nc.tensor.matmul_mx(
+                            out=acc[:],
+                            lhsT=words[:, rows].bitcast(FP8X4),
+                            lhsT_scale=plane[:, rows],
+                            rhs=h_q[b][jc][:, h_cols].bitcast(FP8X4),
+                            rhs_scale=h_s[b][jc][:, h_cols],
+                            start=(b == 0 and side == 0),
+                            stop=(b == PASSES - 1 and side == 1),
+                        )
+                y = ring.tile([P, width], F32, name="y")
+                nc.vector.tensor_tensor(y[:], acc[:], base_t[mt][:, out_cols], ALU.add)
+                squared = ring.tile([P, width], F32, name="squared")
+                nc.scalar.activation(squared[:], y[:], ACT.Square)
+                result = ring.tile([P, width], F32, name="result", bufs=8)
+                weight = wt_t[:, mt : mt + 1]
+                if width == BANK:
+                    nc.gpsimd.tensor_scalar(result[:], squared[:], weight, 0.0, ALU.mult, ALU.add)
+                else:
+                    nc.vector.tensor_scalar(result[:], squared[:], weight, None, ALU.mult)
+                nc.sync.dma_start(out[rows, out_cols], result[:])
 
-        quant_w1(0, 0)
-        quant_w1(1, 0)
-        v_s.append(keep.tile([P, BANK], U8, name="v_s1", tag="g001", align_bytes=64))
-        nc.vector.tensor_copy(v_s[1][:], tab_s[:].indirect(part(1)))
-        for a in range(NP):
-            v_w[a].append(keep.tile([P, BANK], U32, name="v_w1", tag="g10%d" % a, align_bytes=64))
-            nc.vector.tensor_copy(v_w[a][1][:], tab_w[a][:].indirect(part(1)))
-        h_unit(0, 0, 0)
-        h_unit(0, 0, 1)
-        quant_w1(0, 1)
-        low_unit(0)
-        quant_w1(1, 1)
-        h_unit(0, 1, 0)
-        h_unit(0, 1, 1)
-        low_unit(1)
-        h_unit(1, 0, 0)
-        h_unit(1, 0, 1)
-        h_unit(1, 1, 0)
-        h_unit(1, 1, 1)
         for jc in range(2):
-            for mt in range(S2 // P):
-                final(mt, jc)
+            gather(loose_s[jc], tab_s, loose_part(jc))
+        for a in range(PASSES):
+            gather(loose_w[a][0], tab_w[a], loose_part(0))
+            gather(bound_w[a], tab_w[a], bound[:])
+            gather(loose_w[a][1], tab_w[a], loose_part(1))
+            if a == 0:
+                for k_pass in range(PASSES):
+                    cast_w1(k_pass, 0, 0)
+                    cast_w1(k_pass, 0, 1)
+                    quantise_w1(k_pass, 0)
+        nc.vector.tensor_copy(w4_wd[:].bitcast(U16), w4_w[:].bitcast(U16).rearrange("p a (c t) -> p a t c", t=PACK))
+        cast_w1(0, 1, 0)
+        first_h()
+        make_low(0, "right")
+        cast_w1(0, 1, 1)
+        quantise_w1(0, 1)
+        cast_w1(1, 1, 0)
+        cast_w1(1, 1, 1)
+        quantise_w1(1, 1)
+        later_h(0, 1)
+        later_h(1, 0)
+        make_low(1, "left")
+        later_h(1, 1)
+        score(0, BANK, "right")
+        score(BANK, HALF, "left")
+        score(BANK + HALF, HALF, "right")

@@ -263,8 +263,8 @@ def tile_list_watermark_twin_mismatch_kernel(
                 nc.scalar.activation(squared[:], y[:], ACT.Square)
                 result = ring.tile([P, width], F32, name="result", bufs=8)
                 weight = wt_t[:, mt : mt + 1]
-                if width == BANK:
-                    nc.gpsimd.tensor_scalar(result[:], squared[:], weight, 0.0, ALU.mult, ALU.add)
+                if width == BANK and mt % 2 == 0:
+                    nc.scalar.activation(result[:], squared[:], ACT.Copy, scale=weight)
                 else:
                     nc.vector.tensor_scalar(result[:], squared[:], weight, None, ALU.mult)
                 nc.sync.dma_start(out[rows, out_cols], result[:])

from contextlib import ExitStack

import concourse.mybir as mybir

K, T, S, S2 = 1024, 2048, 1024, 512
FLOPS = 2 * K * K * S + 2 * 2 * K * K * S2 + 2 * 2 * K * S2 * S

F32 = mybir.dt.float32
BF16 = mybir.dt.bfloat16
I32 = mybir.dt.int32
U32 = mybir.dt.uint32
U16 = mybir.dt.uint16
U8 = mybir.dt.uint8
FP8X4 = mybir.dt.float8_e4m3fn_x4
FP4X4 = mybir.dt.float4_e2m1fn_x4
ALU = mybir.AluOpType
ACT = mybir.ActivationFunctionType

P = 128
PACK = 4
PASS = P * PACK
PASSES = K // PASS
QUADS = 4
ROWS = 4
BANK = 512
HALF = BANK // 2
RUN = 4
M_TILES = S2 // P
GAIN_ON_SCALAR = (1, 1, 1)


def tile_list_watermark_twin_mismatch_kernel(
    tc, tab_words, tab_scales, offs, offs2, w1, w4_words, w4_scales, gain, neg, base, wt, out
):
    nc = tc.nc
    with ExitStack() as ctx:
        keep = ctx.enter_context(tc.tile_pool(name="keep", bufs=1))
        ring = ctx.enter_context(tc.tile_pool(name="ring", bufs=4))
        psum = ctx.enter_context(tc.psum_pool(name="psum", bufs=4))

        def held(shape, dtype, name):
            return keep.tile(shape, dtype, name=name, align_bytes=64)

        loose = keep.tile([P, S // 16], U16, name="loose")
        bound = keep.tile([P, S2 // 16], U16, name="bound")
        tab_w = [held([P, T], U32, "tab_w%d" % a) for a in range(PASSES)]
        tab_s = held([P, T], U8, "tab_s")
        w4_w = held([P, PASSES, 2 * K], U8, "w4_w")
        w4_s = held([P, PASSES, K], U8, "w4_s")
        w4_wd = held([P, PASSES, PACK, 2 * (K // PACK)], U8, "w4_wd")
        w4_sd = held([P, PASSES, PACK, K // PACK], U8, "w4_sd")
        bound_w = [held([P, S2], U32, "bound_w%d" % a) for a in range(PASSES)]
        bound_s = [held([P, S2], U8, "bound_s%d" % a) for a in range(PASSES)]
        loose_w = [[held([P, BANK], U32, "loose_w%d%d" % (a, jc)) for jc in range(2)] for a in range(PASSES)]
        loose_s = [held([P, BANK], U8, "loose_s%d" % jc) for jc in range(2)]
        w1_q = [[held([P, PASS], U32, "w1_q%d%d" % (a, b)) for b in range(PASSES)] for a in range(PASSES)]
        w1_s = [[held([P, PASS], U8, "w1_s%d%d" % (a, b)) for b in range(PASSES)] for a in range(PASSES)]
        h_q = [[held([P, BANK], U32, "h_q%d%d" % (b, jc)) for jc in range(2)] for b in range(PASSES)]
        h_s = [[held([P, BANK], U8, "h_s%d%d" % (b, jc)) for jc in range(2)] for b in range(PASSES)]
        low_q = [held([P, S2], U32, "low_q%d" % b) for b in range(PASSES)]
        low_s = [held([P, S2], U8, "low_s%d" % b) for b in range(PASSES)]
        gain_t = held([P, PASSES, PACK], F32, "gain_t")
        neg_t = held([P, PASSES, PACK], F32, "neg_t")
        wt_t = held([P, M_TILES], F32, "wt_t")
        base_t = [held([P, S], F32, "base%d" % mt) for mt in range(M_TILES)]
        warm_in = held([P, 1], F32, "warm_in")
        warm_out = held([P, 1], F32, "warm_out")
        w1_raw = {}
        w1_grouped = [
            [held([P, PACK, P, PACK], BF16, "w1_grouped%d%d" % (a, b)) for b in range(PASSES)] for a in range(PASSES)
        ]

        nc.vector.memset(tab_s[:].bitcast(I32), 0)
        nc.vector.memset(warm_in[:], 0.0)
        nc.scalar.activation(warm_out[:], warm_in[:], ACT.Sin)
        nc.vector.memset(w4_s[:].rearrange("p a n -> p (a n)").bitcast(I32), 0)
        nc.vector.memset(bound_s[1][:].bitcast(I32), 0)

        def load_planes(tile, scales):
            for q in range(QUADS):
                rows = tile[32 * q : 32 * q + ROWS * PASSES, :]
                nc.sync.dma_start(rows.bitcast(I32), scales[:, ROWS * q : ROWS * (q + 1), :].bitcast(I32))

        def lift_plane(lifted, both):
            for q in range(QUADS):
                nc.sync.dma_start(
                    lifted[32 * q : 32 * q + ROWS].bitcast(I32), both[32 * q + ROWS : 32 * q + 2 * ROWS].bitcast(I32)
                )

        def load_tab(a):
            nc.sync.dma_start(tab_w[a][:].bitcast(I32), tab_words[a].rearrange("p t i -> p (t i)").bitcast(I32))

        def load_w1(a, b, half):
            raw = held([P, PACK, HALF], F32, "w1_raw%d%d%d" % (a, b, half))
            first_col = b * PASS + half * HALF
            block = w1[a * PASS : (a + 1) * PASS, first_col : first_col + HALF]
            nc.sync.dma_start(raw[:], block.rearrange("(p i) c -> p i c", i=PACK))
            w1_raw[(a, b, half)] = raw

        def gather(picked, window, offsets):
            nc.vector.tensor_copy(picked[:], window[:].indirect(offsets))

        def loose_part(jc):
            return loose[:, jc * (BANK // 16) : (jc + 1) * (BANK // 16)]

        nc.sync.dma_start(bound[:], offs2)
        load_planes(tab_s, tab_scales)
        nc.sync.dma_start(loose[:], offs)
        load_tab(0)
        load_w1(0, 0, 0)
        load_w1(0, 0, 1)
        for q in range(QUADS):
            rows = w4_scales[:, ROWS * q : ROWS * (q + 1), :].rearrange("a r n -> r a n")
            nc.sync.dma_start(w4_s[32 * q : 32 * q + ROWS, :, :].bitcast(I32), rows.bitcast(I32))
        load_w1(1, 0, 0)
        load_w1(1, 0, 1)
        load_tab(1)
        gather(bound_s[0], tab_s, bound[:])
        lift_plane(bound_s[1], bound_s[0])
        load_w1(0, 1, 0)
        nc.vector.tensor_copy(w4_sd[:], w4_s[:].rearrange("p a (c t) -> p a t c", t=PACK))
        nc.sync.dma_start(w4_w[:].bitcast(I32), w4_words.rearrange("a p n -> p a n").bitcast(I32))
        nc.sync.dma_start(gain_t[:], gain.rearrange("(b p t) -> p b t", b=PASSES, t=PACK))
        nc.sync.dma_start(neg_t[:], neg.rearrange("(b p t) -> p b t", b=PASSES, t=PACK))
        load_w1(0, 1, 1)
        load_w1(1, 1, 0)
        load_w1(1, 1, 1)
        for mt in range(M_TILES):
            nc.sync.dma_start(base_t[mt][:], base[mt * P : (mt + 1) * P, :])
        with nc.allow_non_contiguous_dma(reason="one weight a partition"):
            nc.sync.dma_start(wt_t[:], wt.rearrange("(mt p) -> p mt", p=P))

        def cast_w1(a, b, half):
            nc.scalar.copy(
                w1_grouped[a][b][:].rearrange("p t c i -> p c i t")[:, half * P // 2 : (half + 1) * P // 2, :, :],
                w1_raw[(a, b, half)][:].rearrange("p i (c t) -> p c i t", t=PACK),
            )

        def quantise_w1(a, b):
            grouped = w1_grouped[a][b]
            for half in range(2):
                cols = slice(half * HALF, (half + 1) * HALF)
                nc.vector.quantize_mx(
                    out=w1_q[a][b][:, cols].bitcast(FP8X4),
                    scales=w1_s[a][b][:, cols],
                    in_=grouped[:, 2 * half : 2 * half + 2, :, :].rearrange("p t c i -> p (t c i)"),
                )

        def w1_product(acc, b, t, words, planes):
            for a in range(PASSES):
                nc.tensor.matmul_mx(
                    out=acc,
                    lhsT=w1_q[a][b][:, t * P : (t + 1) * P].bitcast(FP8X4),
                    lhsT_scale=w1_s[a][b][:, t * P : (t + 1) * P],
                    rhs=words[a].bitcast(FP8X4),
                    rhs_scale=planes[ROWS * a : P],
                    start=(a == 0),
                    stop=(a == PASSES - 1),
                )

        def woven(tile):
            return tile.rearrange("p (c i) t -> p c t i", i=RUN)

        def by_slice(tile):
            return tile.rearrange("p t (c i) -> p c t i", i=RUN)

        def finish_h(sines, b, jc, half):
            cols = slice(half * HALF, (half + 1) * HALF)
            grouped = ring.tile([P, HALF, PACK], BF16, name="h_grouped", align_bytes=64)
            if (b, jc, half) == GAIN_ON_SCALAR:
                scaled = held([P, PACK, HALF], BF16, "scaled")
                for t in range(PACK):
                    nc.scalar.activation(scaled[:, t, :], sines[:, t, :], ACT.Copy, scale=gain_t[:, b, t : t + 1])
                nc.scalar.copy(woven(grouped[:]), by_slice(scaled[:]))
            else:
                gains = gain_t[:, b, :].unsqueeze(1).unsqueeze(3).to_broadcast([P, HALF // RUN, PACK, RUN])
                nc.vector.tensor_tensor(woven(grouped[:]), by_slice(sines), gains, ALU.mult)
            nc.vector.quantize_mx(
                out=h_q[b][jc][:, cols].bitcast(FP8X4),
                scales=h_s[b][jc][:, cols],
                in_=grouped[:].rearrange("p n t -> p (n t)"),
            )

        def first_h():
            sines = held([P, PACK, BANK], F32, "w1_raw010")
            for t in range(PACK):
                acc = psum.tile([P, BANK], F32, name="left")
                w1_product(acc[:], 0, t, [loose_w[a][0][:] for a in range(PASSES)], loose_s[0][:])
                nc.scalar.activation(sines[:, t, :], acc[:], ACT.Sin)
            for half in range(2):
                finish_h(sines[:, :, half * HALF : (half + 1) * HALF], 0, 0, half)

        def later_h(b, jc):
            for half in range(2):
                cols = slice(half * HALF, (half + 1) * HALF)
                sines = ring.tile([P, PACK, HALF], F32, name="sines", bufs=5)
                for pair in range(2):
                    acc = psum.tile([P, 2, HALF], F32, name="left")
                    for t in (2 * pair, 2 * pair + 1):
                        words = [loose_w[a][jc][:, cols] for a in range(PASSES)]
                        w1_product(acc[:, t % 2, :], b, t, words, loose_s[jc][:, cols])
                    nc.scalar.activation(sines[:, 2 * pair : 2 * pair + 2, :], acc[:], ACT.Sin)
                finish_h(sines[:], b, jc, half)

        def make_low(b, w1_banks):
            negated = ring.tile([P, PACK, S2], F32, name="negated", bufs=2)
            for t in range(PACK):
                acc = psum.tile([P, S2], F32, name=w1_banks)
                w1_product(acc[:], b, t, [bound_w[a][:] for a in range(PASSES)], bound_s[0][:])
                nc.scalar.activation(negated[:, t, :], acc[:], ACT.Copy, scale=neg_t[:, b, t : t + 1])
            w4_sums = []
            for mt in range(M_TILES):
                acc = psum.tile([P, PACK, P], F32, name="right")
                cols = slice(mt * P, (mt + 1) * P)
                for t in range(PACK):
                    for a in range(PASSES):
                        nc.tensor.matmul_mx(
                            out=acc[:, t, :],
                            lhsT=w4_wd[:, a, t, 2 * b * P : 2 * (b + 1) * P].bitcast(FP4X4),
                            lhsT_scale=w4_sd[:, a, t, b * P : (b + 1) * P],
                            rhs=bound_w[a][:, cols].bitcast(FP8X4),
                            rhs_scale=bound_s[a][:, cols],
                            start=(a == 0),
                            stop=(a == PASSES - 1),
                        )
                w4_sums.append(acc)
            grouped = ring.tile([P, S2, PACK], BF16, name="low_grouped", bufs=2, align_bytes=64)
            for mt in range(M_TILES):
                cols = slice(mt * P, (mt + 1) * P)
                nc.vector.tensor_tensor(
                    woven(grouped[:, cols, :]), by_slice(w4_sums[mt][:]), by_slice(negated[:, :, cols]), ALU.min
                )
            for half in range(2):
                cols = slice(half * HALF, (half + 1) * HALF)
                nc.vector.quantize_mx(
                    out=low_q[b][:, cols].bitcast(FP8X4),
                    scales=low_s[b][:, cols],
                    in_=grouped[:, cols, :].rearrange("p n t -> p (n t)"),
                )

        def score(first_col, width, banks):
            jc = first_col // BANK
            h_cols = slice(first_col % BANK, first_col % BANK + width)
            out_cols = slice(first_col, first_col + width)
            for mt in range(M_TILES):
                rows = slice(mt * P, (mt + 1) * P)
                acc = psum.tile([P, width], F32, name=banks)
                for b in range(PASSES):
                    sides = ((bound_w[b], bound_s[0][ROWS * b : P]), (low_q[b], low_s[b][:]))
                    for side, (words, plane) in enumerate(sides):
                        nc.tensor.matmul_mx(
                            out=acc[:],
                            lhsT=words[:, rows].bitcast(FP8X4),
                            lhsT_scale=plane[:, rows],
                            rhs=h_q[b][jc][:, h_cols].bitcast(FP8X4),
                            rhs_scale=h_s[b][jc][:, h_cols],
                            start=(b == 0 and side == 0),
                            stop=(b == PASSES - 1 and side == 1),
                        )
                y = ring.tile([P, width], F32, name="y")
                nc.vector.tensor_tensor(y[:], acc[:], base_t[mt][:, out_cols], ALU.add)
                squared = ring.tile([P, width], F32, name="squared")
                nc.scalar.activation(squared[:], y[:], ACT.Square)
                result = ring.tile([P, width], F32, name="result", bufs=8)
                weight = wt_t[:, mt : mt + 1]
                if width == BANK and mt % 2 == 0:
                    nc.scalar.activation(result[:], squared[:], ACT.Copy, scale=weight)
                else:
                    nc.vector.tensor_scalar(result[:], squared[:], weight, None, ALU.mult)
                nc.sync.dma_start(out[rows, out_cols], result[:])

        for jc in range(2):
            gather(loose_s[jc], tab_s, loose_part(jc))
        for a in range(PASSES):
            gather(loose_w[a][0], tab_w[a], loose_part(0))
            gather(bound_w[a], tab_w[a], bound[:])
            gather(loose_w[a][1], tab_w[a], loose_part(1))
            if a == 0:
                for k_pass in range(PASSES):
                    cast_w1(k_pass, 0, 0)
                    cast_w1(k_pass, 0, 1)
                    quantise_w1(k_pass, 0)
        nc.vector.tensor_copy(w4_wd[:].bitcast(U16), w4_w[:].bitcast(U16).rearrange("p a (c t) -> p a t c", t=PACK))
        cast_w1(0, 1, 0)
        first_h()
        make_low(0, "right")
        cast_w1(0, 1, 1)
        quantise_w1(0, 1)
        cast_w1(1, 1, 0)
        cast_w1(1, 1, 1)
        quantise_w1(1, 1)
        later_h(0, 1)
        later_h(1, 0)
        make_low(1, "left")
        later_h(1, 1)
        score(0, BANK, "right")
        score(BANK, HALF, "left")
        score(BANK + HALF, HALF, "right")
